import numpy as np
import ml_dtypes


def mxq(x, axis, fmt="e4m3"):
    dtype, down = {"e4m3": (ml_dtypes.float8_e4m3fn, 7), "e5m2": (ml_dtypes.float8_e5m2, 14)}[fmt]
    v = np.moveaxis(np.asarray(x, np.float32).astype(ml_dtypes.bfloat16).astype(np.float64), axis, -1)
    blocks = v.reshape(v.shape[:-1] + (-1, 32))
    amax = np.abs(blocks).max(-1, keepdims=True)
    byte = np.maximum(np.where(amax > 0, np.frexp(amax)[1] - 1 + 127, 0) - down, 1)
    scale = np.exp2(byte - 127.0)
    codes = (blocks / scale).astype(np.float32).astype(dtype).astype(np.float64)
    return np.moveaxis((codes * scale).reshape(v.shape), -1, axis)


WIDE = False


def mx_kscale(k):
    if not WIDE:
        return np.ones(k)
    levels = np.array([10, -10, 5, -5, 0])
    if k % 512:
        return np.exp2(np.random.permutation(np.resize(levels, k // 32))).repeat(32)
    a = np.empty((k // 512, 16))
    for p in range(k // 512):
        a[p, :8] = np.random.permutation(np.resize(levels, 8))
        for g in range(8):
            far = levels[np.abs(levels - a[p, g]) >= 10]
            a[p, g + 8] = far[np.random.randint(len(far))]
    return np.exp2(a.ravel()).repeat(32)


def f64(x):
    return np.asarray(x).astype(np.float64)


E2M1 = np.array([0.0, 0.5, 1.0, 1.5, 2.0, 3.0, 4.0, 6.0, -0.0, -0.5, -1.0, -1.5, -2.0, -3.0, -4.0, -6.0])


def pack_weight(w, fmt):
    k, n = w.shape
    w = f64(np.asarray(w, np.float32).astype(ml_dtypes.bfloat16)).reshape(k // 32, 32, n)
    amax = np.abs(w).max(1)
    if fmt == "e4m3":
        byte = np.frexp(amax)[1] - 1 + 127 - 7
    else:
        mant, ex = np.frexp(amax / 6.0)
        byte = np.where(mant > 0.5, ex, ex - 1) + 127
    byte = np.clip(np.where(amax > 0, byte, 1), 1, 254)
    scaled = (w * np.exp2(127.0 - byte)[:, None, :]).reshape(k, n).astype(np.float32)
    by_word = np.ascontiguousarray(scaled.reshape(k // 512, 128, 4, n).transpose(0, 1, 3, 2))
    if fmt == "e4m3":
        words = by_word.astype(ml_dtypes.float8_e4m3fn).view(np.uint8)
    else:
        c = by_word.astype(ml_dtypes.float4_e2m1fn).view(np.uint8) & 0xF
        words = (c[..., 0::2] | (c[..., 1::2] << 4)).reshape(k // 512, 128, 2 * n)
    return np.ascontiguousarray(words), np.ascontiguousarray(byte.astype(np.uint8).reshape(k // 512, 16, n))


def unpack_weight(words, scales, fmt):
    g, _, n = scales.shape
    words = np.ascontiguousarray(words).reshape(g, 128, n, -1)
    if fmt == "e4m3":
        vals = words.view(ml_dtypes.float8_e4m3fn).astype(np.float64)
    else:
        nib = np.empty((g, 128, n, 4), np.uint8)
        nib[..., 0::2] = words & 0xF
        nib[..., 1::2] = words >> 4
        vals = E2M1[nib]
    vals = vals * np.repeat(np.exp2(scales.astype(np.float64) - 127.0), 8, axis=1)[..., None]
    return vals.transpose(0, 1, 3, 2).reshape(g * 512, n)


def bf(x):
    return np.asarray(x, np.float32).astype(ml_dtypes.bfloat16)


def planes(Y):
    r, m = Y.shape
    b = f64(bf(Y)).reshape(r // 32, 32, m)
    amax = np.abs(b).max(1)
    byte = np.clip(np.where(amax > 0, np.frexp(amax)[1] - 1 + 127 - 7, 1), 1, 254)
    codes = (b * np.exp2(127.0 - byte)[:, None, :]).reshape(r, m).astype(np.float32).astype(ml_dtypes.float8_e4m3fn).view(np.uint8)
    words = codes.reshape(r // 512, 128, 4, m).transpose(0, 1, 3, 2)
    return np.ascontiguousarray(words), np.ascontiguousarray(byte.astype(np.uint8).reshape(r // 512, 16, m))


K, L, T, N = 1024, 512, 512, 512


def setup_inputs():
    n = np.random.standard_normal
    fk = mx_kscale(K)
    fl = mx_kscale(L)
    wap = pack_weight(n((K, N)) * 1 / np.sqrt(K) * fk[:, None], "e2m1")
    xsp = pack_weight(n((L, T)) / fl[:, None], "e4m3")
    wsp = pack_weight(n((L, N)) * 1 / np.sqrt(L) * fl[:, None], "e2m1")
    wcp = pack_weight(n((K, N)) * 1 / np.sqrt(K) * fk[:, None], "e4m3")
    return {
        "xt": (n((K, T)) * np.random.uniform(0.3, 1.7, (1, T)) / fk[:, None]).astype(np.float32),
        "wa_words": wap[0],
        "wa_scales": wap[1],
        "xs_words": xsp[0],
        "xs_scales": xsp[1],
        "ws_words": wsp[0],
        "ws_scales": wsp[1],
        "wc_words": wcp[0],
        "wc_scales": wcp[1],
        "bi": (np.random.uniform(-0.8, 0.8, (1, N))).astype(np.float32),
    }


def reference(xt, wa_words, wa_scales, xs_words, xs_scales, ws_words, ws_scales, wc_words, wc_scales, bi):
    wau = unpack_weight(wa_words, wa_scales, "e2m1")
    xsu = unpack_weight(xs_words, xs_scales, "e4m3")
    wsu = unpack_weight(ws_words, ws_scales, "e2m1")
    wcu = unpack_weight(wc_words, wc_scales, "e4m3")
    xtq = mxq(f64(xt), 0, "e4m3")
    a0 = xtq.T @ wau + xsu.T @ wsu
    b0 = xtq.T @ wcu
    a = a0 + f64(bi)
    b = b0 + f64(bi)
    s = np.tanh(2.0 * np.mean(a * b, axis=1, keepdims=True))
    y = a + s * b
    words, scales = planes(y)
    return y, words, scales

@@ -1,0 +1,245 @@
+from contextlib import ExitStack
+
+import concourse.mybir as mybir
+from concourse.masks import make_identity
+
+K, L, T, N = 1024, 512, 512, 512
+FLOPS = 2 * T * N * (K + L + K)
+
+F32 = mybir.dt.float32
+BF16 = mybir.dt.bfloat16
+I32 = mybir.dt.int32
+U32 = mybir.dt.uint32
+U8 = mybir.dt.uint8
+FP8X4 = mybir.dt.float8_e4m3fn_x4
+FP4X4 = mybir.dt.float4_e2m1fn_x4
+ACT = mybir.ActivationFunctionType
+ALU = mybir.AluOpType
+
+P = 128
+PACK = 4
+QUADS = 4
+CH = 128
+GP_TILES = 0
+
+
+def tile_mix_rows_heard_by_agreement_pl_kernel(
+    tc, xt, wa_words, wa_scales, xs_words, xs_scales, ws_words, ws_scales, wc_words, wc_scales, bi,
+    out_0, out_1, out_2,
+):
+    nc = tc.nc
+    with ExitStack() as ctx:
+        sb = ctx.enter_context(tc.tile_pool(name="sb", bufs=1))
+        psum = ctx.enter_context(tc.psum_pool(name="psum", bufs=1))
+        ctx.enter_context(tc.manual_schedule())
+
+        def sbt(name, shape, dtype):
+            return sb.tile(shape, dtype, name=name, align_bytes=64)
+
+        xs_raw = sbt("xs_raw", [P, T], I32)
+        xs_codes = sbt("xs_codes", [P, T], I32)
+        xs_sc_raw = sbt("xs_sc_raw", [P, T], U8)
+        xs_sc = sbt("xs_sc", [P, T], U8)
+        wc = [sbt("wc%d" % z, [P, N], I32) for z in range(2)]
+        wc_sc = sbt("wc_sc", [P, N], U8)
+        wa = sbt("wa", [P, 2, 2 * N], U8)
+        wa_sc = sbt("wa_sc", [P, 2, N], U8)
+        ws = sbt("ws", [P, 2 * N], U8)
+        ws_sc = sbt("ws_sc", [P, N], U8)
+        x0 = sbt("x0", [P, PACK, T], F32)
+        x1 = [sbt("x1_%d" % h, [P, PACK, T // 2], F32) for h in range(2)]
+        xb = [sbt("xb%d" % z, [P, PACK, P, PACK], BF16) for z in range(2)]
+        x_codes = [[sbt("xc%d_%d" % (z, r), [P, P], U32) for r in range(PACK)] for z in range(2)]
+        x_sc = [[sbt("xsc%d_%d" % (z, r), [P, P], U8) for r in range(PACK)] for z in range(2)]
+        bi_col = sbt("bi_col", [P, PACK], F32)
+        bi_row = sbt("bi_row", [P, N], F32)
+        ident = sbt("ident", [P, P], F32)
+        warm = sbt("warm", [P, 1], F32)
+
+        nc.scalar.dma_start(out=bi_col[:], in_=bi.rearrange("o (p c) -> (o p) c", c=PACK))
+        nc.vector.memset(wc_sc[:].bitcast(U32), 0)
+        nc.vector.memset(warm[:], 0.0)
+        nc.vector.memset(ws_sc[:].bitcast(U32), 0)
+        nc.vector.memset(wa_sc[:].rearrange("p z n -> p (z n)").bitcast(U32), 0)
+        nc.scalar.activation(out=warm[:], in_=warm[:], func=ACT.Tanh)
+        nc.gpsimd.memset(xs_sc_raw[:].bitcast(U32), 0)
+        make_identity(nc, ident[:])
+        for q in range(QUADS):
+            nc.gpsimd.dma_start(out=xs_sc_raw[32 * q : 32 * q + 4, :].bitcast(I32),
+                                in_=xs_scales[0, 4 * q : 4 * q + 4, :].bitcast(I32))
+
+        def words(ap):
+            return ap.rearrange("p n t -> p (n t)").bitcast(I32)
+
+        def ld_ws_sc(q):
+            nc.sync.dma_start(out=ws_sc[32 * q : 32 * q + 4, :].bitcast(I32),
+                              in_=ws_scales[0, 4 * q : 4 * q + 4, :].bitcast(I32))
+
+        def ld_wa_sc(q):
+            nc.sync.dma_start(out=wa_sc[32 * q : 32 * q + 4, :, :].bitcast(I32),
+                              in_=wa_scales[:, 4 * q : 4 * q + 4, :].rearrange("z r c -> r z c").bitcast(I32))
+
+        def ld_x1(h):
+            nc.sync.dma_start(out=x1[h][:],
+                              in_=xt[512:1024, 256 * h : 256 * h + 256].rearrange("(p j) t -> p j t", j=PACK))
+
+        nc.sync.dma_start(out=xs_raw[:], in_=words(xs_words[0]))
+        nc.sync.dma_start(out=wc[0][:], in_=words(wc_words[0]))
+        for q in range(QUADS):
+            nc.sync.dma_start(out=wc_sc[32 * q + 4 : 32 * q + 12, :].bitcast(I32),
+                              in_=wc_scales[:, 4 * q : 4 * q + 4, :].bitcast(I32))
+        nc.sync.dma_start(out=x0[:], in_=xt[0:512, :].rearrange("(p j) t -> p j t", j=PACK))
+        ld_x1(0)
+        for q in range(QUADS):
+            ld_ws_sc(q)
+        ld_x1(1)
+        nc.sync.dma_start(out=wc[1][:], in_=words(wc_words[1]))
+        ld_wa_sc(0)
+        ld_wa_sc(1)
+        nc.sync.dma_start(out=wa[:].bitcast(I32), in_=wa_words.rearrange("z p c -> p z c").bitcast(I32))
+        ld_wa_sc(2)
+        ld_wa_sc(3)
+        nc.sync.dma_start(out=ws[:].bitcast(I32), in_=ws_words[0].bitcast(I32))
+
+        bi_ps = psum.tile([P, PACK, P], F32, name="bi_ps", tag="a3")
+        for c in range(PACK):
+            nc.tensor.transpose(bi_ps[:, c, :], bi_col[:, c : c + 1].to_broadcast([P, P]), ident[:])
+        nc.scalar.copy(out=bi_row[:].rearrange("p (q c) -> p q c", c=PACK), in_=bi_ps[:].rearrange("p c q -> p q c"))
+
+        nc.vector.tensor_copy(out=xs_codes[:].rearrange("p (r m) -> p m r", r=PACK),
+                              in_=xs_raw[:].rearrange("p (m r) -> p m r", r=PACK))
+
+        def cast(z, raw, m_base, m_count, m_vec):
+            src = raw[:].rearrange("p j (m r) -> p m r j", r=PACK)
+            dst = xb[z][:].rearrange("p r m j -> p m r j")
+            nc.scalar.copy(out=dst[:, m_base + m_vec : m_base + m_count], in_=src[:, m_vec:m_count])
+            nc.vector.tensor_copy(out=dst[:, m_base : m_base + m_vec], in_=src[:, 0:m_vec])
+
+        def quant(z, r):
+            nc.vector.quantize_mx(out=x_codes[z][r][:].bitcast(FP8X4), scales=x_sc[z][r][:],
+                                  in_=xb[z][:, r].rearrange("p m j -> p (m j)"))
+
+        a_ps = [psum.tile([P, N], F32, name="a_ps%d" % r, tag="a%d" % r) for r in range(PACK)]
+        b_ps = [psum.tile([P, N], F32, name="b_ps%d" % r, tag="b%d" % r) for r in range(PACK)]
+
+        def mm_b(z, r):
+            nc.tensor.matmul_mx(out=b_ps[r][:], lhsT=x_codes[z][r][:].bitcast(FP8X4), lhsT_scale=x_sc[z][r][:],
+                                rhs=wc[z][:].bitcast(FP8X4), rhs_scale=wc_sc[4 + 4 * z : P, :],
+                                start=(z == 0), stop=(z == 1))
+
+        def mm_a(r):
+            for z in range(2):
+                nc.tensor.matmul_mx(out=a_ps[r][:], lhsT=x_codes[z][r][:].bitcast(FP8X4), lhsT_scale=x_sc[z][r][:],
+                                    rhs=wa[:, z, :].bitcast(FP4X4), rhs_scale=wa_sc[:, z, :],
+                                    start=(z == 0), stop=False)
+            cols = slice(P * r, P * r + P)
+            nc.tensor.matmul_mx(out=a_ps[r][:], lhsT=xs_codes[:, cols].bitcast(FP8X4), lhsT_scale=xs_sc[:, cols],
+                                rhs=ws[:].bitcast(FP4X4), rhs_scale=ws_sc[:], start=False, stop=True)
+
+        cast(0, x0, 0, 128, 84)
+        for r in range(PACK):
+            quant(0, r)
+            mm_b(0, r)
+        cast(1, x1[0], 0, 64, 44)
+        nc.vector.tensor_copy(out=xs_sc[:].rearrange("p (r m) -> p r m", r=PACK),
+                              in_=xs_sc_raw[:].rearrange("p (m r) -> p r m", r=PACK))
+        cast(1, x1[1], 64, 64, 44)
+        for r in range(PACK):
+            quant(1, r)
+        mm_b(1, 0)
+        mm_b(1, 1)
+        mm_a(0)
+        mm_b(1, 2)
+        mm_a(1)
+        mm_b(1, 3)
+        mm_a(2)
+        mm_a(3)
+
+        a_sb = [sbt("a_sb%d" % r, [P, N], F32) for r in range(PACK)]
+        b_sb = [sbt("b_sb%d" % r, [P, N], F32) for r in range(PACK)]
+        prod = [sbt("prod%d" % r, [P, N], F32) for r in range(PACK)]
+        junk = sbt("junk", [P, N], F32)
+        dot = [sbt("dot%d" % r, [P, 1], F32) for r in range(PACK)]
+        s = [sbt("s%d" % r, [P, 1], F32) for r in range(PACK)]
+        nch = N // CH
+        y = [sbt("y%d" % c, [P, PACK, CH], F32) for c in range(nch)]
+        yb = [sbt("yb%d" % c, [P, CH, PACK], BF16) for c in range(nch)]
+        o_codes = sbt("o_codes", [P, N], U32)
+        o_sc = sbt("o_sc", [P, N], U8)
+
+        def add_a(r):
+            nc.vector.tensor_tensor(out=a_sb[r][:], in0=a_ps[r][:], in1=bi_row[:], op=ALU.add)
+
+        def add_b(r):
+            nc.vector.tensor_tensor(out=b_sb[r][:], in0=b_ps[r][:], in1=bi_row[:], op=ALU.add)
+
+        def agree(r):
+            if r < GP_TILES:
+                nc.gpsimd.tensor_tensor(out=prod[r][:], in0=a_sb[r][:], in1=b_sb[r][:], op=ALU.mult)
+                nc.scalar.activation(out=junk[:], in_=prod[r][:], func=ACT.Copy, accum_out=dot[r][:])
+            else:
+                nc.vector.scalar_tensor_tensor(out=prod[r][:], in0=a_sb[r][:], scalar=1.0, in1=b_sb[r][:],
+                                               op0=ALU.mult, op1=ALU.mult, accum_out=dot[r][:])
+            nc.scalar.activation(out=s[r][:], in_=dot[r][:], func=ACT.Tanh, scale=2.0 / N)
+
+        def mix(r, c):
+            cols = slice(CH * c, CH * c + CH)
+            nc.vector.scalar_tensor_tensor(out=y[c][:, r, :], in0=b_sb[r][:, cols], scalar=s[r][:],
+                                           in1=a_sb[r][:, cols], op0=ALU.mult, op1=ALU.add)
+
+        out_rows = out_0.rearrange("(p r) n -> p r n", r=PACK)
+
+        def store_y(c):
+            nc.sync.dma_start(out=out_rows[:, :, CH * c : CH * c + CH], in_=y[c][:])
+
+        def round_y(c, eng):
+            eng(out=yb[c][:], in_=y[c][:].rearrange("p r c -> p c r"))
+
+        def quant_y(c):
+            cols = slice(CH * c, CH * c + CH)
+            nc.vector.quantize_mx(out=o_codes[:, cols].bitcast(FP8X4), scales=o_sc[:, cols],
+                                  in_=yb[c][:].rearrange("p c r -> p (c r)"))
+
+        def store_words(c0, c1):
+            nc.sync.dma_start(out=words(out_1[0])[:, c0:c1], in_=o_codes[:, c0:c1].bitcast(I32))
+
+        add_b(0)
+        add_b(1)
+        add_a(0)
+        add_b(2)
+        agree(0)
+        add_a(1)
+        add_b(3)
+        agree(1)
+        add_a(2)
+        mix(0, 0)
+        mix(0, 1)
+        agree(2)
+        add_a(3)
+        mix(0, 2)
+        mix(0, 3)
+        agree(3)
+        mix(1, 0)
+        mix(2, 0)
+        mix(1, 1)
+        mix(2, 1)
+        for c in range(nch):
+            if c >= 2:
+                mix(1, c)
+                mix(2, c)
+            mix(3, c)
+            store_y(c)
+            if c < nch - 1:
+                round_y(c, nc.scalar.copy)
+            if c >= 1 and c < nch - 1:
+                quant_y(c - 1)
+        quant_y(nch - 2)
+        store_words(0, 3 * CH)
+        round_y(nch - 1, nc.vector.tensor_copy)
+        quant_y(nch - 1)
+        store_words(3 * CH, N)
+
+        for q in range(QUADS):
+            eng = nc.sync if q % 2 == 0 else nc.scalar
+            eng.dma_start(out=out_2[0, 4 * q : 4 * q + 4, :].bitcast(I32),
+                          in_=o_sc[32 * q : 32 * q + 4, :].bitcast(I32))

@@ -57,23 +57,23 @@ def tile_mix_rows_heard_by_agreement_pl_kernel(
         warm = sbt("warm", [P, 1], F32)
 
         nc.scalar.dma_start(out=bi_col[:], in_=bi.rearrange("o (p c) -> (o p) c", c=PACK))
-        nc.vector.memset(wc_sc[:].bitcast(U32), 0)
+        nc.vector.memset(xs_sc_raw[:].bitcast(U32), 0)
         nc.vector.memset(warm[:], 0.0)
-        nc.vector.memset(ws_sc[:].bitcast(U32), 0)
+        nc.vector.memset(wc_sc[:].bitcast(U32), 0)
         nc.vector.memset(wa_sc[:].rearrange("p z n -> p (z n)").bitcast(U32), 0)
         nc.scalar.activation(out=warm[:], in_=warm[:], func=ACT.Tanh)
-        nc.gpsimd.memset(xs_sc_raw[:].bitcast(U32), 0)
+        nc.gpsimd.memset(ws_sc[:].bitcast(U32), 0)
         make_identity(nc, ident[:])
         for q in range(QUADS):
-            nc.gpsimd.dma_start(out=xs_sc_raw[32 * q : 32 * q + 4, :].bitcast(I32),
-                                in_=xs_scales[0, 4 * q : 4 * q + 4, :].bitcast(I32))
+            nc.gpsimd.dma_start(out=ws_sc[32 * q : 32 * q + 4, :].bitcast(I32),
+                                in_=ws_scales[0, 4 * q : 4 * q + 4, :].bitcast(I32))
 
         def words(ap):
             return ap.rearrange("p n t -> p (n t)").bitcast(I32)
 
-        def ld_ws_sc(q):
-            nc.sync.dma_start(out=ws_sc[32 * q : 32 * q + 4, :].bitcast(I32),
-                              in_=ws_scales[0, 4 * q : 4 * q + 4, :].bitcast(I32))
+        def ld_xs_sc(q):
+            nc.sync.dma_start(out=xs_sc_raw[32 * q : 32 * q + 4, :].bitcast(I32),
+                              in_=xs_scales[0, 4 * q : 4 * q + 4, :].bitcast(I32))
 
         def ld_wa_sc(q):
             nc.sync.dma_start(out=wa_sc[32 * q : 32 * q + 4, :, :].bitcast(I32),
@@ -86,19 +86,17 @@ def tile_mix_rows_heard_by_agreement_pl_kernel(
         nc.sync.dma_start(out=xs_raw[:], in_=words(xs_words[0]))
         nc.sync.dma_start(out=wc[0][:], in_=words(wc_words[0]))
         for q in range(QUADS):
+            ld_xs_sc(q)
+        nc.sync.dma_start(out=x0[:], in_=xt[0:512, :].rearrange("(p j) t -> p j t", j=PACK))
+        for q in range(QUADS):
             nc.sync.dma_start(out=wc_sc[32 * q + 4 : 32 * q + 12, :].bitcast(I32),
                               in_=wc_scales[:, 4 * q : 4 * q + 4, :].bitcast(I32))
-        nc.sync.dma_start(out=x0[:], in_=xt[0:512, :].rearrange("(p j) t -> p j t", j=PACK))
         ld_x1(0)
-        for q in range(QUADS):
-            ld_ws_sc(q)
         ld_x1(1)
         nc.sync.dma_start(out=wc[1][:], in_=words(wc_words[1]))
-        ld_wa_sc(0)
-        ld_wa_sc(1)
+        for q in range(QUADS):
+            ld_wa_sc(q)
         nc.sync.dma_start(out=wa[:].bitcast(I32), in_=wa_words.rearrange("z p c -> p z c").bitcast(I32))
-        ld_wa_sc(2)
-        ld_wa_sc(3)
         nc.sync.dma_start(out=ws[:].bitcast(I32), in_=ws_words[0].bitcast(I32))
 
         bi_ps = psum.tile([P, PACK, P], F32, name="bi_ps", tag="a3")
@@ -108,6 +106,8 @@ def tile_mix_rows_heard_by_agreement_pl_kernel(
 
         nc.vector.tensor_copy(out=xs_codes[:].rearrange("p (r m) -> p m r", r=PACK),
                               in_=xs_raw[:].rearrange("p (m r) -> p m r", r=PACK))
+        nc.vector.tensor_copy(out=xs_sc[:].rearrange("p (r m) -> p r m", r=PACK),
+                              in_=xs_sc_raw[:].rearrange("p (m r) -> p r m", r=PACK))
 
         def cast(z, raw, m_base, m_count, m_vec):
             src = raw[:].rearrange("p j (m r) -> p m r j", r=PACK)
@@ -141,8 +141,6 @@ def tile_mix_rows_heard_by_agreement_pl_kernel(
             quant(0, r)
             mm_b(0, r)
         cast(1, x1[0], 0, 64, 44)
-        nc.vector.tensor_copy(out=xs_sc[:].rearrange("p (r m) -> p r m", r=PACK),
-                              in_=xs_sc_raw[:].rearrange("p (m r) -> p r m", r=PACK))
         cast(1, x1[1], 64, 64, 44)
         for r in range(PACK):
             quant(1, r)

@@ -20,7 +20,7 @@ P = 128
 PACK = 4
 QUADS = 4
 CH = 128
-GP_TILES = 0
+GP_TILES = 2
 
 
 def tile_mix_rows_heard_by_agreement_pl_kernel(
@@ -48,7 +48,8 @@ def tile_mix_rows_heard_by_agreement_pl_kernel(
         ws_sc = sbt("ws_sc", [P, N], U8)
         x0 = sbt("x0", [P, PACK, T], F32)
         x1 = [sbt("x1_%d" % h, [P, PACK, T // 2], F32) for h in range(2)]
-        xb = [sbt("xb%d" % z, [P, PACK, P, PACK], BF16) for z in range(2)]
+        xb0 = sbt("xb0", [P, PACK, P, PACK], BF16)
+        xb1 = [sbt("xb1_%d" % h, [P, PACK, P // 2, PACK], BF16) for h in range(2)]
         x_codes = [[sbt("xc%d_%d" % (z, r), [P, P], U32) for r in range(PACK)] for z in range(2)]
         x_sc = [[sbt("xsc%d_%d" % (z, r), [P, P], U8) for r in range(PACK)] for z in range(2)]
         bi_col = sbt("bi_col", [P, PACK], F32)
@@ -109,15 +110,16 @@ def tile_mix_rows_heard_by_agreement_pl_kernel(
         nc.vector.tensor_copy(out=xs_sc[:].rearrange("p (r m) -> p r m", r=PACK),
                               in_=xs_sc_raw[:].rearrange("p (m r) -> p r m", r=PACK))
 
-        def cast(z, raw, m_base, m_count, m_vec):
+        def cast(raw, xb, m_vec):
             src = raw[:].rearrange("p j (m r) -> p m r j", r=PACK)
-            dst = xb[z][:].rearrange("p r m j -> p m r j")
-            nc.scalar.copy(out=dst[:, m_base + m_vec : m_base + m_count], in_=src[:, m_vec:m_count])
-            nc.vector.tensor_copy(out=dst[:, m_base : m_base + m_vec], in_=src[:, 0:m_vec])
+            dst = xb[:].rearrange("p r m j -> p m r j")
+            nc.scalar.copy(out=dst[:, m_vec:], in_=src[:, m_vec:])
+            nc.vector.tensor_copy(out=dst[:, 0:m_vec], in_=src[:, 0:m_vec])
 
-        def quant(z, r):
-            nc.vector.quantize_mx(out=x_codes[z][r][:].bitcast(FP8X4), scales=x_sc[z][r][:],
-                                  in_=xb[z][:, r].rearrange("p m j -> p (m j)"))
+        def quant(z, r, xb, m0):
+            cols = slice(m0, m0 + xb.shape[2])
+            nc.vector.quantize_mx(out=x_codes[z][r][:, cols].bitcast(FP8X4), scales=x_sc[z][r][:, cols],
+                                  in_=xb[:, r].rearrange("p m j -> p (m j)"))
 
         a_ps = [psum.tile([P, N], F32, name="a_ps%d" % r, tag="a%d" % r) for r in range(PACK)]
         b_ps = [psum.tile([P, N], F32, name="b_ps%d" % r, tag="b%d" % r) for r in range(PACK)]
@@ -136,14 +138,14 @@ def tile_mix_rows_heard_by_agreement_pl_kernel(
             nc.tensor.matmul_mx(out=a_ps[r][:], lhsT=xs_codes[:, cols].bitcast(FP8X4), lhsT_scale=xs_sc[:, cols],
                                 rhs=ws[:].bitcast(FP4X4), rhs_scale=ws_sc[:], start=False, stop=True)
 
-        cast(0, x0, 0, 128, 84)
+        cast(x0, xb0, 84)
         for r in range(PACK):
-            quant(0, r)
+            quant(0, r, xb0, 0)
             mm_b(0, r)
-        cast(1, x1[0], 0, 64, 44)
-        cast(1, x1[1], 64, 64, 44)
-        for r in range(PACK):
-            quant(1, r)
+        for h in range(2):
+            cast(x1[h], xb1[h], 44)
+            for r in range(PACK):
+                quant(1, r, xb1[h], 64 * h)
         mm_b(1, 0)
         mm_b(1, 1)
         mm_a(0)
@@ -204,25 +206,24 @@ def tile_mix_rows_heard_by_agreement_pl_kernel(
         add_b(0)
         add_b(1)
         add_a(0)
-        add_b(2)
         agree(0)
+        add_b(2)
         add_a(1)
-        add_b(3)
         agree(1)
+        add_b(3)
         add_a(2)
-        mix(0, 0)
-        mix(0, 1)
-        agree(2)
         add_a(3)
-        mix(0, 2)
-        mix(0, 3)
+        agree(2)
         agree(3)
+        mix(0, 0)
         mix(1, 0)
-        mix(2, 0)
+        mix(0, 1)
         mix(1, 1)
+        mix(2, 0)
         mix(2, 1)
         for c in range(nch):
             if c >= 2:
+                mix(0, c)
                 mix(1, c)
                 mix(2, c)
             mix(3, c)

@@ -19,6 +19,7 @@ ALU = mybir.AluOpType
 P = 128
 PACK = 4
 QUADS = 4
+WARM = 0
 CH = 128
 GP_TILES = 2
 
@@ -110,11 +111,12 @@ def tile_mix_rows_heard_by_agreement_pl_kernel(
         nc.vector.tensor_copy(out=xs_sc[:].rearrange("p (r m) -> p r m", r=PACK),
                               in_=xs_sc_raw[:].rearrange("p (m r) -> p r m", r=PACK))
 
-        def cast(raw, xb, m_vec):
-            src = raw[:].rearrange("p j (m r) -> p m r j", r=PACK)
-            dst = xb[:].rearrange("p r m j -> p m r j")
-            nc.scalar.copy(out=dst[:, m_vec:], in_=src[:, m_vec:])
-            nc.vector.tensor_copy(out=dst[:, 0:m_vec], in_=src[:, 0:m_vec])
+        def cast(raw, xb, m_vec, r_step):
+            src = raw[:].rearrange("p j (m r) -> p m j r", r=PACK)
+            dst = xb[:].rearrange("p r m j -> p m j r")
+            for r0 in range(0, PACK, r_step):
+                nc.scalar.copy(out=dst[:, m_vec:, :, r0 : r0 + r_step], in_=src[:, m_vec:, :, r0 : r0 + r_step])
+                nc.vector.tensor_copy(out=dst[:, 0:m_vec, :, r0 : r0 + r_step], in_=src[:, 0:m_vec, :, r0 : r0 + r_step])
 
         def quant(z, r, xb, m0):
             cols = slice(m0, m0 + xb.shape[2])
@@ -138,12 +140,15 @@ def tile_mix_rows_heard_by_agreement_pl_kernel(
             nc.tensor.matmul_mx(out=a_ps[r][:], lhsT=xs_codes[:, cols].bitcast(FP8X4), lhsT_scale=xs_sc[:, cols],
                                 rhs=ws[:].bitcast(FP4X4), rhs_scale=ws_sc[:], start=False, stop=True)
 
-        cast(x0, xb0, 84)
+        for i in range(WARM):
+            nc.tensor.matmul_mx(out=a_ps[i % 2][:], lhsT=xs_raw[:, 0:P].bitcast(FP8X4), lhsT_scale=xs_sc_raw[:, 0:P],
+                                rhs=xs_raw[:].bitcast(FP8X4), rhs_scale=xs_sc_raw[:], start=True, stop=True)
+        cast(x0, xb0, 84, 2)
         for r in range(PACK):
             quant(0, r, xb0, 0)
             mm_b(0, r)
         for h in range(2):
-            cast(x1[h], xb1[h], 44)
+            cast(x1[h], xb1[h], 44, 2)
             for r in range(PACK):
                 quant(1, r, xb1[h], 64 * h)
         mm_b(1, 0)
@@ -161,9 +166,8 @@ def tile_mix_rows_heard_by_agreement_pl_kernel(
         junk = sbt("junk", [P, N], F32)
         dot = [sbt("dot%d" % r, [P, 1], F32) for r in range(PACK)]
         s = [sbt("s%d" % r, [P, 1], F32) for r in range(PACK)]
-        nch = N // CH
-        y = [sbt("y%d" % c, [P, PACK, CH], F32) for c in range(nch)]
-        yb = [sbt("yb%d" % c, [P, CH, PACK], BF16) for c in range(nch)]
+        y = sbt("y", [P, PACK, N], F32)
+        yb = sbt("yb", [P, N, PACK], BF16)
         o_codes = sbt("o_codes", [P, N], U32)
         o_sc = sbt("o_sc", [P, N], U8)
 
@@ -182,23 +186,22 @@ def tile_mix_rows_heard_by_agreement_pl_kernel(
                                                op0=ALU.mult, op1=ALU.mult, accum_out=dot[r][:])
             nc.scalar.activation(out=s[r][:], in_=dot[r][:], func=ACT.Tanh, scale=2.0 / N)
 
-        def mix(r, c):
-            cols = slice(CH * c, CH * c + CH)
-            nc.vector.scalar_tensor_tensor(out=y[c][:, r, :], in0=b_sb[r][:, cols], scalar=s[r][:],
-                                           in1=a_sb[r][:, cols], op0=ALU.mult, op1=ALU.add)
+        def mix(r, c0, c1):
+            nc.vector.scalar_tensor_tensor(out=y[:, r, c0:c1], in0=b_sb[r][:, c0:c1], scalar=s[r][:],
+                                           in1=a_sb[r][:, c0:c1], op0=ALU.mult, op1=ALU.add)
 
         out_rows = out_0.rearrange("(p r) n -> p r n", r=PACK)
 
-        def store_y(c):
-            nc.sync.dma_start(out=out_rows[:, :, CH * c : CH * c + CH], in_=y[c][:])
+        def store_y(r0, r1, c0, c1):
+            nc.sync.dma_start(out=out_rows[:, r0:r1, c0:c1], in_=y[:, r0:r1, c0:c1])
 
-        def round_y(c, eng):
-            eng(out=yb[c][:], in_=y[c][:].rearrange("p r c -> p c r"))
+        def round_y(eng, c0, c1):
+            eng(out=yb[:, c0:c1, :].rearrange("p (c i) r -> p c r i", i=PACK),
+                in_=y[:, :, c0:c1].rearrange("p r (c i) -> p c r i", i=PACK))
 
-        def quant_y(c):
-            cols = slice(CH * c, CH * c + CH)
-            nc.vector.quantize_mx(out=o_codes[:, cols].bitcast(FP8X4), scales=o_sc[:, cols],
-                                  in_=yb[c][:].rearrange("p c r -> p (c r)"))
+        def quant_y(c0, c1):
+            nc.vector.quantize_mx(out=o_codes[:, c0:c1].bitcast(FP8X4), scales=o_sc[:, c0:c1],
+                                  in_=yb[:, c0:c1, :].rearrange("p c r -> p (c r)"))
 
         def store_words(c0, c1):
             nc.sync.dma_start(out=words(out_1[0])[:, c0:c1], in_=o_codes[:, c0:c1].bitcast(I32))
@@ -213,30 +216,29 @@ def tile_mix_rows_heard_by_agreement_pl_kernel(
         add_b(3)
         add_a(2)
         add_a(3)
+        mix(0, 0, N)
+        store_y(0, 1, 0, N)
         agree(2)
         agree(3)
-        mix(0, 0)
-        mix(1, 0)
-        mix(0, 1)
-        mix(1, 1)
-        mix(2, 0)
-        mix(2, 1)
-        for c in range(nch):
-            if c >= 2:
-                mix(0, c)
-                mix(1, c)
-                mix(2, c)
-            mix(3, c)
-            store_y(c)
-            if c < nch - 1:
-                round_y(c, nc.scalar.copy)
-            if c >= 1 and c < nch - 1:
-                quant_y(c - 1)
-        quant_y(nch - 2)
-        store_words(0, 3 * CH)
-        round_y(nch - 1, nc.vector.tensor_copy)
-        quant_y(nch - 1)
-        store_words(3 * CH, N)
+        mix(1, 0, N)
+        store_y(1, 2, 0, N)
+        mix(2, 0, 128)
+        mix(3, 0, 128)
+        round_y(nc.scalar.copy, 0, 128)
+        mix(2, 128, 256)
+        mix(3, 128, 256)
+        round_y(nc.scalar.copy, 128, 256)
+        store_y(2, 4, 0, 256)
+        mix(2, 256, N)
+        mix(3, 256, N)
+        store_y(2, 4, 256, N)
+        round_y(nc.scalar.copy, 256, 320)
+        quant_y(0, 128)
+        round_y(nc.vector.tensor_copy, 320, N)
+        quant_y(128, 256)
+        store_words(0, 256)
+        quant_y(256, N)
+        store_words(256, N)
 
         for q in range(QUADS):
             eng = nc.sync if q % 2 == 0 else nc.scalar

@@ -19,9 +19,16 @@ ALU = mybir.AluOpType
 P = 128
 PACK = 4
 QUADS = 4
-WARM = 0
-CH = 128
+K_PASS = P * PACK
+PASSES = K // K_PASS
+HALF_T = T // 2
+HALF_M = P // 2
+TILE_PAIR = 2
 GP_TILES = 2
+GP_SCALE_LOADS = 3
+VEC_M_FIRST = 84
+VEC_M_SECOND = (24, 40)
+CUT_1, CUT_2, CUT_3 = 128, 256, 320
 
 
 def tile_mix_rows_heard_by_agreement_pl_kernel(
@@ -41,22 +48,31 @@ def tile_mix_rows_heard_by_agreement_pl_kernel(
         xs_codes = sbt("xs_codes", [P, T], I32)
         xs_sc_raw = sbt("xs_sc_raw", [P, T], U8)
         xs_sc = sbt("xs_sc", [P, T], U8)
-        wc = [sbt("wc%d" % z, [P, N], I32) for z in range(2)]
+        wc = [sbt("wc%d" % z, [P, N], I32) for z in range(PASSES)]
         wc_sc = sbt("wc_sc", [P, N], U8)
-        wa = sbt("wa", [P, 2, 2 * N], U8)
-        wa_sc = sbt("wa_sc", [P, 2, N], U8)
+        wa = sbt("wa", [P, PASSES, 2 * N], U8)
+        wa_sc = sbt("wa_sc", [P, PASSES, N], U8)
         ws = sbt("ws", [P, 2 * N], U8)
         ws_sc = sbt("ws_sc", [P, N], U8)
         x0 = sbt("x0", [P, PACK, T], F32)
-        x1 = [sbt("x1_%d" % h, [P, PACK, T // 2], F32) for h in range(2)]
+        x1 = [sbt("x1_%d" % h, [P, PACK, HALF_T], F32) for h in range(2)]
         xb0 = sbt("xb0", [P, PACK, P, PACK], BF16)
-        xb1 = [sbt("xb1_%d" % h, [P, PACK, P // 2, PACK], BF16) for h in range(2)]
-        x_codes = [[sbt("xc%d_%d" % (z, r), [P, P], U32) for r in range(PACK)] for z in range(2)]
-        x_sc = [[sbt("xsc%d_%d" % (z, r), [P, P], U8) for r in range(PACK)] for z in range(2)]
+        xb1 = [sbt("xb1_%d" % h, [P, PACK, HALF_M, PACK], BF16) for h in range(2)]
+        x_codes = [[sbt("xc%d_%d" % (z, r), [P, P], U32) for r in range(PACK)] for z in range(PASSES)]
+        x_sc = [[sbt("xsc%d_%d" % (z, r), [P, P], U8) for r in range(PACK)] for z in range(PASSES)]
         bi_col = sbt("bi_col", [P, PACK], F32)
         bi_row = sbt("bi_row", [P, N], F32)
         ident = sbt("ident", [P, P], F32)
         warm = sbt("warm", [P, 1], F32)
+
+        def words(ap):
+            return ap.rearrange("p n t -> p (n t)").bitcast(I32)
+
+        def live(q):
+            return slice(32 * q, 32 * q + 4)
+
+        def rows(q):
+            return slice(4 * q, 4 * q + 4)
 
         nc.scalar.dma_start(out=bi_col[:], in_=bi.rearrange("o (p c) -> (o p) c", c=PACK))
         nc.vector.memset(xs_sc_raw[:].bitcast(U32), 0)
@@ -66,40 +82,36 @@ def tile_mix_rows_heard_by_agreement_pl_kernel(
         nc.scalar.activation(out=warm[:], in_=warm[:], func=ACT.Tanh)
         nc.gpsimd.memset(ws_sc[:].bitcast(U32), 0)
         make_identity(nc, ident[:])
-        for q in range(QUADS):
-            nc.gpsimd.dma_start(out=ws_sc[32 * q : 32 * q + 4, :].bitcast(I32),
-                                in_=ws_scales[0, 4 * q : 4 * q + 4, :].bitcast(I32))
 
-        def words(ap):
-            return ap.rearrange("p n t -> p (n t)").bitcast(I32)
+        def load_ws_sc(queue, q):
+            queue.dma_start(out=ws_sc[live(q), :].bitcast(I32), in_=ws_scales[0, rows(q), :].bitcast(I32))
 
-        def ld_xs_sc(q):
-            nc.sync.dma_start(out=xs_sc_raw[32 * q : 32 * q + 4, :].bitcast(I32),
-                              in_=xs_scales[0, 4 * q : 4 * q + 4, :].bitcast(I32))
+        def load_wa_sc(q):
+            nc.sync.dma_start(out=wa_sc[live(q), :, :].bitcast(I32),
+                              in_=wa_scales[:, rows(q), :].rearrange("z r c -> r z c").bitcast(I32))
 
-        def ld_wa_sc(q):
-            nc.sync.dma_start(out=wa_sc[32 * q : 32 * q + 4, :, :].bitcast(I32),
-                              in_=wa_scales[:, 4 * q : 4 * q + 4, :].rearrange("z r c -> r z c").bitcast(I32))
-
-        def ld_x1(h):
-            nc.sync.dma_start(out=x1[h][:],
-                              in_=xt[512:1024, 256 * h : 256 * h + 256].rearrange("(p j) t -> p j t", j=PACK))
+        for q in range(GP_SCALE_LOADS):
+            load_ws_sc(nc.gpsimd, q)
 
         nc.sync.dma_start(out=xs_raw[:], in_=words(xs_words[0]))
         nc.sync.dma_start(out=wc[0][:], in_=words(wc_words[0]))
         for q in range(QUADS):
-            ld_xs_sc(q)
-        nc.sync.dma_start(out=x0[:], in_=xt[0:512, :].rearrange("(p j) t -> p j t", j=PACK))
+            nc.sync.dma_start(out=xs_sc_raw[live(q), :].bitcast(I32), in_=xs_scales[0, rows(q), :].bitcast(I32))
+        nc.sync.dma_start(out=x0[:], in_=xt[0:K_PASS, :].rearrange("(p j) t -> p j t", j=PACK))
         for q in range(QUADS):
-            nc.sync.dma_start(out=wc_sc[32 * q + 4 : 32 * q + 12, :].bitcast(I32),
-                              in_=wc_scales[:, 4 * q : 4 * q + 4, :].bitcast(I32))
-        ld_x1(0)
-        ld_x1(1)
+            nc.sync.dma_start(out=wc_sc[32 * q + 4 : 32 * q + 4 + 4 * PASSES, :].bitcast(I32),
+                              in_=wc_scales[:, rows(q), :].bitcast(I32))
+        load_wa_sc(0)
+        for h in range(2):
+            nc.sync.dma_start(out=x1[h][:],
+                              in_=xt[K_PASS:K, HALF_T * h : HALF_T * (h + 1)].rearrange("(p j) t -> p j t", j=PACK))
         nc.sync.dma_start(out=wc[1][:], in_=words(wc_words[1]))
-        for q in range(QUADS):
-            ld_wa_sc(q)
+        for q in range(1, QUADS):
+            load_wa_sc(q)
         nc.sync.dma_start(out=wa[:].bitcast(I32), in_=wa_words.rearrange("z p c -> p z c").bitcast(I32))
         nc.sync.dma_start(out=ws[:].bitcast(I32), in_=ws_words[0].bitcast(I32))
+        for q in range(GP_SCALE_LOADS, QUADS):
+            load_ws_sc(nc.sync, q)
 
         bi_ps = psum.tile([P, PACK, P], F32, name="bi_ps", tag="a3")
         for c in range(PACK):
@@ -111,14 +123,15 @@ def tile_mix_rows_heard_by_agreement_pl_kernel(
         nc.vector.tensor_copy(out=xs_sc[:].rearrange("p (r m) -> p r m", r=PACK),
                               in_=xs_sc_raw[:].rearrange("p (m r) -> p r m", r=PACK))
 
-        def cast(raw, xb, m_vec, r_step):
+        def round_x(raw, xb, m_vec):
             src = raw[:].rearrange("p j (m r) -> p m j r", r=PACK)
             dst = xb[:].rearrange("p r m j -> p m j r")
-            for r0 in range(0, PACK, r_step):
-                nc.scalar.copy(out=dst[:, m_vec:, :, r0 : r0 + r_step], in_=src[:, m_vec:, :, r0 : r0 + r_step])
-                nc.vector.tensor_copy(out=dst[:, 0:m_vec, :, r0 : r0 + r_step], in_=src[:, 0:m_vec, :, r0 : r0 + r_step])
+            for r0 in range(0, PACK, TILE_PAIR):
+                pair = slice(r0, r0 + TILE_PAIR)
+                nc.scalar.copy(out=dst[:, m_vec:, :, pair], in_=src[:, m_vec:, :, pair])
+                nc.vector.tensor_copy(out=dst[:, 0:m_vec, :, pair], in_=src[:, 0:m_vec, :, pair])
 
-        def quant(z, r, xb, m0):
+        def quantise_x(z, r, xb, m0):
             cols = slice(m0, m0 + xb.shape[2])
             nc.vector.quantize_mx(out=x_codes[z][r][:, cols].bitcast(FP8X4), scales=x_sc[z][r][:, cols],
                                   in_=xb[:, r].rearrange("p m j -> p (m j)"))
@@ -126,13 +139,13 @@ def tile_mix_rows_heard_by_agreement_pl_kernel(
         a_ps = [psum.tile([P, N], F32, name="a_ps%d" % r, tag="a%d" % r) for r in range(PACK)]
         b_ps = [psum.tile([P, N], F32, name="b_ps%d" % r, tag="b%d" % r) for r in range(PACK)]
 
-        def mm_b(z, r):
+        def matmul_b(z, r):
             nc.tensor.matmul_mx(out=b_ps[r][:], lhsT=x_codes[z][r][:].bitcast(FP8X4), lhsT_scale=x_sc[z][r][:],
                                 rhs=wc[z][:].bitcast(FP8X4), rhs_scale=wc_sc[4 + 4 * z : P, :],
-                                start=(z == 0), stop=(z == 1))
+                                start=(z == 0), stop=(z == PASSES - 1))
 
-        def mm_a(r):
-            for z in range(2):
+        def matmul_a(r):
+            for z in range(PASSES):
                 nc.tensor.matmul_mx(out=a_ps[r][:], lhsT=x_codes[z][r][:].bitcast(FP8X4), lhsT_scale=x_sc[z][r][:],
                                     rhs=wa[:, z, :].bitcast(FP4X4), rhs_scale=wa_sc[:, z, :],
                                     start=(z == 0), stop=False)
@@ -140,25 +153,20 @@ def tile_mix_rows_heard_by_agreement_pl_kernel(
             nc.tensor.matmul_mx(out=a_ps[r][:], lhsT=xs_codes[:, cols].bitcast(FP8X4), lhsT_scale=xs_sc[:, cols],
                                 rhs=ws[:].bitcast(FP4X4), rhs_scale=ws_sc[:], start=False, stop=True)
 
-        for i in range(WARM):
-            nc.tensor.matmul_mx(out=a_ps[i % 2][:], lhsT=xs_raw[:, 0:P].bitcast(FP8X4), lhsT_scale=xs_sc_raw[:, 0:P],
-                                rhs=xs_raw[:].bitcast(FP8X4), rhs_scale=xs_sc_raw[:], start=True, stop=True)
-        cast(x0, xb0, 84, 2)
+        round_x(x0, xb0, VEC_M_FIRST)
         for r in range(PACK):
-            quant(0, r, xb0, 0)
-            mm_b(0, r)
+            quantise_x(0, r, xb0, 0)
+            matmul_b(0, r)
         for h in range(2):
-            cast(x1[h], xb1[h], 44, 2)
+            round_x(x1[h], xb1[h], VEC_M_SECOND[h])
             for r in range(PACK):
-                quant(1, r, xb1[h], 64 * h)
-        mm_b(1, 0)
-        mm_b(1, 1)
-        mm_a(0)
-        mm_b(1, 2)
-        mm_a(1)
-        mm_b(1, 3)
-        mm_a(2)
-        mm_a(3)
+                quantise_x(1, r, xb1[h], HALF_M * h)
+
+        matmul_b(1, 0)
+        for r in range(PACK):
+            if r + 1 < PACK:
+                matmul_b(1, r + 1)
+            matmul_a(r)
 
         a_sb = [sbt("a_sb%d" % r, [P, N], F32) for r in range(PACK)]
         b_sb = [sbt("b_sb%d" % r, [P, N], F32) for r in range(PACK)]
@@ -195,11 +203,11 @@ def tile_mix_rows_heard_by_agreement_pl_kernel(
         def store_y(r0, r1, c0, c1):
             nc.sync.dma_start(out=out_rows[:, r0:r1, c0:c1], in_=y[:, r0:r1, c0:c1])
 
-        def round_y(eng, c0, c1):
-            eng(out=yb[:, c0:c1, :].rearrange("p (c i) r -> p c r i", i=PACK),
-                in_=y[:, :, c0:c1].rearrange("p r (c i) -> p c r i", i=PACK))
+        def round_y(copy, c0, c1):
+            copy(out=yb[:, c0:c1, :].rearrange("p (c i) r -> p c r i", i=PACK),
+                 in_=y[:, :, c0:c1].rearrange("p r (c i) -> p c r i", i=PACK))
 
-        def quant_y(c0, c1):
+        def quantise_y(c0, c1):
             nc.vector.quantize_mx(out=o_codes[:, c0:c1].bitcast(FP8X4), scales=o_sc[:, c0:c1],
                                   in_=yb[:, c0:c1, :].rearrange("p c r -> p (c r)"))
 
@@ -207,40 +215,36 @@ def tile_mix_rows_heard_by_agreement_pl_kernel(
             nc.sync.dma_start(out=words(out_1[0])[:, c0:c1], in_=o_codes[:, c0:c1].bitcast(I32))
 
         add_b(0)
-        add_b(1)
-        add_a(0)
-        agree(0)
-        add_b(2)
-        add_a(1)
-        agree(1)
-        add_b(3)
-        add_a(2)
-        add_a(3)
+        for r in range(PACK):
+            if r + 1 < PACK:
+                add_b(r + 1)
+            add_a(r)
+            if r < GP_TILES:
+                agree(r)
+
         mix(0, 0, N)
         store_y(0, 1, 0, N)
-        agree(2)
-        agree(3)
+        for r in range(GP_TILES, PACK):
+            agree(r)
         mix(1, 0, N)
         store_y(1, 2, 0, N)
-        mix(2, 0, 128)
-        mix(3, 0, 128)
-        round_y(nc.scalar.copy, 0, 128)
-        mix(2, 128, 256)
-        mix(3, 128, 256)
-        round_y(nc.scalar.copy, 128, 256)
-        store_y(2, 4, 0, 256)
-        mix(2, 256, N)
-        mix(3, 256, N)
-        store_y(2, 4, 256, N)
-        round_y(nc.scalar.copy, 256, 320)
-        quant_y(0, 128)
-        round_y(nc.vector.tensor_copy, 320, N)
-        quant_y(128, 256)
-        store_words(0, 256)
-        quant_y(256, N)
-        store_words(256, N)
+
+        for c0, c1 in ((0, CUT_1), (CUT_1, CUT_2)):
+            mix(2, c0, c1)
+            mix(3, c0, c1)
+            round_y(nc.scalar.copy, c0, c1)
+        store_y(2, PACK, 0, CUT_2)
+        mix(2, CUT_2, N)
+        mix(3, CUT_2, N)
+        store_y(2, PACK, CUT_2, N)
+        round_y(nc.scalar.copy, CUT_2, CUT_3)
+        quantise_y(0, CUT_1)
+        round_y(nc.vector.tensor_copy, CUT_3, N)
+        quantise_y(CUT_1, CUT_2)
+        store_words(0, CUT_2)
+        quantise_y(CUT_2, N)
+        store_words(CUT_2, N)
 
         for q in range(QUADS):
-            eng = nc.sync if q % 2 == 0 else nc.scalar
-            eng.dma_start(out=out_2[0, 4 * q : 4 * q + 4, :].bitcast(I32),
-                          in_=o_sc[32 * q : 32 * q + 4, :].bitcast(I32))
+            queue = nc.sync if q % 2 == 0 else nc.scalar
+            queue.dma_start(out=out_2[0, rows(q), :].bitcast(I32), in_=o_sc[live(q), :].bitcast(I32))

from contextlib import ExitStack

import concourse.mybir as mybir
from concourse.masks import make_identity

K, L, T, N = 1024, 512, 512, 512
FLOPS = 2 * T * N * (K + L + K)

F32 = mybir.dt.float32
BF16 = mybir.dt.bfloat16
I32 = mybir.dt.int32
U32 = mybir.dt.uint32
U8 = mybir.dt.uint8
FP8X4 = mybir.dt.float8_e4m3fn_x4
FP4X4 = mybir.dt.float4_e2m1fn_x4
ACT = mybir.ActivationFunctionType
ALU = mybir.AluOpType

P = 128
PACK = 4
QUADS = 4
K_PASS = P * PACK
PASSES = K // K_PASS
HALF_T = T // 2
HALF_M = P // 2
TILE_PAIR = 2
GP_TILES = 2
GP_SCALE_LOADS = 3
VEC_M_FIRST = 84
VEC_M_SECOND = (24, 40)
CUT_1, CUT_2, CUT_3 = 128, 256, 320


def tile_mix_rows_heard_by_agreement_pl_kernel(
    tc, xt, wa_words, wa_scales, xs_words, xs_scales, ws_words, ws_scales, wc_words, wc_scales, bi,
    out_0, out_1, out_2,
):
    nc = tc.nc
    with ExitStack() as ctx:
        sb = ctx.enter_context(tc.tile_pool(name="sb", bufs=1))
        psum = ctx.enter_context(tc.psum_pool(name="psum", bufs=1))
        ctx.enter_context(tc.manual_schedule())

        def sbt(name, shape, dtype):
            return sb.tile(shape, dtype, name=name, align_bytes=64)

        xs_raw = sbt("xs_raw", [P, T], I32)
        xs_codes = sbt("xs_codes", [P, T], I32)
        xs_sc_raw = sbt("xs_sc_raw", [P, T], U8)
        xs_sc = sbt("xs_sc", [P, T], U8)
        wc = [sbt("wc%d" % z, [P, N], I32) for z in range(PASSES)]
        wc_sc = sbt("wc_sc", [P, N], U8)
        wa = sbt("wa", [P, PASSES, 2 * N], U8)
        wa_sc = sbt("wa_sc", [P, PASSES, N], U8)
        ws = sbt("ws", [P, 2 * N], U8)
        ws_sc = sbt("ws_sc", [P, N], U8)
        x0 = sbt("x0", [P, PACK, T], F32)
        x1 = [sbt("x1_%d" % h, [P, PACK, HALF_T], F32) for h in range(2)]
        xb0 = sbt("xb0", [P, PACK, P, PACK], BF16)
        xb1 = [sbt("xb1_%d" % h, [P, PACK, HALF_M, PACK], BF16) for h in range(2)]
        x_codes = [[sbt("xc%d_%d" % (z, r), [P, P], U32) for r in range(PACK)] for z in range(PASSES)]
        x_sc = [[sbt("xsc%d_%d" % (z, r), [P, P], U8) for r in range(PACK)] for z in range(PASSES)]
        bi_col = sbt("bi_col", [P, PACK], F32)
        bi_row = sbt("bi_row", [P, N], F32)
        ident = sbt("ident", [P, P], F32)
        warm = sbt("warm", [P, 1], F32)

        def words(ap):
            return ap.rearrange("p n t -> p (n t)").bitcast(I32)

        def live(q):
            return slice(32 * q, 32 * q + 4)

        def rows(q):
            return slice(4 * q, 4 * q + 4)

        nc.scalar.dma_start(out=bi_col[:], in_=bi.rearrange("o (p c) -> (o p) c", c=PACK))
        nc.vector.memset(xs_sc_raw[:].bitcast(U32), 0)
        nc.vector.memset(warm[:], 0.0)
        nc.vector.memset(wc_sc[:].bitcast(U32), 0)
        nc.vector.memset(wa_sc[:].rearrange("p z n -> p (z n)").bitcast(U32), 0)
        nc.scalar.activation(out=warm[:], in_=warm[:], func=ACT.Tanh)
        nc.gpsimd.memset(ws_sc[:].bitcast(U32), 0)
        make_identity(nc, ident[:])

        def load_ws_sc(queue, q):
            queue.dma_start(out=ws_sc[live(q), :].bitcast(I32), in_=ws_scales[0, rows(q), :].bitcast(I32))

        def load_wa_sc(q):
            nc.sync.dma_start(out=wa_sc[live(q), :, :].bitcast(I32),
                              in_=wa_scales[:, rows(q), :].rearrange("z r c -> r z c").bitcast(I32))

        for q in range(GP_SCALE_LOADS):
            load_ws_sc(nc.gpsimd, q)

        nc.sync.dma_start(out=xs_raw[:], in_=words(xs_words[0]))
        nc.sync.dma_start(out=wc[0][:], in_=words(wc_words[0]))
        for q in range(QUADS):
            nc.sync.dma_start(out=xs_sc_raw[live(q), :].bitcast(I32), in_=xs_scales[0, rows(q), :].bitcast(I32))
        nc.sync.dma_start(out=x0[:], in_=xt[0:K_PASS, :].rearrange("(p j) t -> p j t", j=PACK))
        for q in range(QUADS):
            nc.sync.dma_start(out=wc_sc[32 * q + 4 : 32 * q + 4 + 4 * PASSES, :].bitcast(I32),
                              in_=wc_scales[:, rows(q), :].bitcast(I32))
        load_wa_sc(0)
        for h in range(2):
            nc.sync.dma_start(out=x1[h][:],
                              in_=xt[K_PASS:K, HALF_T * h : HALF_T * (h + 1)].rearrange("(p j) t -> p j t", j=PACK))
        nc.sync.dma_start(out=wc[1][:], in_=words(wc_words[1]))
        for q in range(1, QUADS):
            load_wa_sc(q)
        nc.sync.dma_start(out=wa[:].bitcast(I32), in_=wa_words.rearrange("z p c -> p z c").bitcast(I32))
        nc.sync.dma_start(out=ws[:].bitcast(I32), in_=ws_words[0].bitcast(I32))
        for q in range(GP_SCALE_LOADS, QUADS):
            load_ws_sc(nc.sync, q)

        bi_ps = psum.tile([P, PACK, P], F32, name="bi_ps", tag="a3")
        for c in range(PACK):
            nc.tensor.transpose(bi_ps[:, c, :], bi_col[:, c : c + 1].to_broadcast([P, P]), ident[:])
        nc.scalar.copy(out=bi_row[:].rearrange("p (q c) -> p q c", c=PACK), in_=bi_ps[:].rearrange("p c q -> p q c"))

        nc.vector.tensor_copy(out=xs_codes[:].rearrange("p (r m) -> p m r", r=PACK),
                              in_=xs_raw[:].rearrange("p (m r) -> p m r", r=PACK))
        nc.vector.tensor_copy(out=xs_sc[:].rearrange("p (r m) -> p r m", r=PACK),
                              in_=xs_sc_raw[:].rearrange("p (m r) -> p r m", r=PACK))

        def round_x(raw, xb, m_vec):
            src = raw[:].rearrange("p j (m r) -> p m j r", r=PACK)
            dst = xb[:].rearrange("p r m j -> p m j r")
            for r0 in range(0, PACK, TILE_PAIR):
                pair = slice(r0, r0 + TILE_PAIR)
                nc.scalar.copy(out=dst[:, m_vec:, :, pair], in_=src[:, m_vec:, :, pair])
                nc.vector.tensor_copy(out=dst[:, 0:m_vec, :, pair], in_=src[:, 0:m_vec, :, pair])

        def quantise_x(z, r, xb, m0):
            cols = slice(m0, m0 + xb.shape[2])
            nc.vector.quantize_mx(out=x_codes[z][r][:, cols].bitcast(FP8X4), scales=x_sc[z][r][:, cols],
                                  in_=xb[:, r].rearrange("p m j -> p (m j)"))

        a_ps = [psum.tile([P, N], F32, name="a_ps%d" % r, tag="a%d" % r) for r in range(PACK)]
        b_ps = [psum.tile([P, N], F32, name="b_ps%d" % r, tag="b%d" % r) for r in range(PACK)]

        def matmul_b(z, r):
            nc.tensor.matmul_mx(out=b_ps[r][:], lhsT=x_codes[z][r][:].bitcast(FP8X4), lhsT_scale=x_sc[z][r][:],
                                rhs=wc[z][:].bitcast(FP8X4), rhs_scale=wc_sc[4 + 4 * z : P, :],
                                start=(z == 0), stop=(z == PASSES - 1))

        def matmul_a(r):
            for z in range(PASSES):
                nc.tensor.matmul_mx(out=a_ps[r][:], lhsT=x_codes[z][r][:].bitcast(FP8X4), lhsT_scale=x_sc[z][r][:],
                                    rhs=wa[:, z, :].bitcast(FP4X4), rhs_scale=wa_sc[:, z, :],
                                    start=(z == 0), stop=False)
            cols = slice(P * r, P * r + P)
            nc.tensor.matmul_mx(out=a_ps[r][:], lhsT=xs_codes[:, cols].bitcast(FP8X4), lhsT_scale=xs_sc[:, cols],
                                rhs=ws[:].bitcast(FP4X4), rhs_scale=ws_sc[:], start=False, stop=True)

        round_x(x0, xb0, VEC_M_FIRST)
        for r in range(PACK):
            quantise_x(0, r, xb0, 0)
            matmul_b(0, r)
        for h in range(2):
            round_x(x1[h], xb1[h], VEC_M_SECOND[h])
            for r in range(PACK):
                quantise_x(1, r, xb1[h], HALF_M * h)

        matmul_b(1, 0)
        for r in range(PACK):
            if r + 1 < PACK:
                matmul_b(1, r + 1)
            matmul_a(r)

        a_sb = [sbt("a_sb%d" % r, [P, N], F32) for r in range(PACK)]
        b_sb = [sbt("b_sb%d" % r, [P, N], F32) for r in range(PACK)]
        prod = [sbt("prod%d" % r, [P, N], F32) for r in range(PACK)]
        junk = sbt("junk", [P, N], F32)
        dot = [sbt("dot%d" % r, [P, 1], F32) for r in range(PACK)]
        s = [sbt("s%d" % r, [P, 1], F32) for r in range(PACK)]
        y = sbt("y", [P, PACK, N], F32)
        yb = sbt("yb", [P, N, PACK], BF16)
        o_codes = sbt("o_codes", [P, N], U32)
        o_sc = sbt("o_sc", [P, N], U8)

        def add_a(r):
            nc.vector.tensor_tensor(out=a_sb[r][:], in0=a_ps[r][:], in1=bi_row[:], op=ALU.add)

        def add_b(r):
            nc.vector.tensor_tensor(out=b_sb[r][:], in0=b_ps[r][:], in1=bi_row[:], op=ALU.add)

        def agree(r):
            if r < GP_TILES:
                nc.gpsimd.tensor_tensor(out=prod[r][:], in0=a_sb[r][:], in1=b_sb[r][:], op=ALU.mult)
                nc.scalar.activation(out=junk[:], in_=prod[r][:], func=ACT.Copy, accum_out=dot[r][:])
            else:
                nc.vector.scalar_tensor_tensor(out=prod[r][:], in0=a_sb[r][:], scalar=1.0, in1=b_sb[r][:],
                                               op0=ALU.mult, op1=ALU.mult, accum_out=dot[r][:])
            nc.scalar.activation(out=s[r][:], in_=dot[r][:], func=ACT.Tanh, scale=2.0 / N)

        def mix(r, c0, c1):
            nc.vector.scalar_tensor_tensor(out=y[:, r, c0:c1], in0=b_sb[r][:, c0:c1], scalar=s[r][:],
                                           in1=a_sb[r][:, c0:c1], op0=ALU.mult, op1=ALU.add)

        out_rows = out_0.rearrange("(p r) n -> p r n", r=PACK)

        def store_y(r0, r1, c0, c1):
            nc.sync.dma_start(out=out_rows[:, r0:r1, c0:c1], in_=y[:, r0:r1, c0:c1])

        def round_y(copy, c0, c1):
            copy(out=yb[:, c0:c1, :].rearrange("p (c i) r -> p c r i", i=PACK),
                 in_=y[:, :, c0:c1].rearrange("p r (c i) -> p c r i", i=PACK))

        def quantise_y(c0, c1):
            nc.vector.quantize_mx(out=o_codes[:, c0:c1].bitcast(FP8X4), scales=o_sc[:, c0:c1],
                                  in_=yb[:, c0:c1, :].rearrange("p c r -> p (c r)"))

        def store_words(c0, c1):
            nc.sync.dma_start(out=words(out_1[0])[:, c0:c1], in_=o_codes[:, c0:c1].bitcast(I32))

        add_b(0)
        for r in range(PACK):
            if r + 1 < PACK:
                add_b(r + 1)
            add_a(r)
            if r < GP_TILES:
                agree(r)

        mix(0, 0, N)
        store_y(0, 1, 0, N)
        for r in range(GP_TILES, PACK):
            agree(r)
        mix(1, 0, N)
        store_y(1, 2, 0, N)

        for c0, c1 in ((0, CUT_1), (CUT_1, CUT_2)):
            mix(2, c0, c1)
            mix(3, c0, c1)
            round_y(nc.scalar.copy, c0, c1)
        store_y(2, PACK, 0, CUT_2)
        mix(2, CUT_2, N)
        mix(3, CUT_2, N)
        store_y(2, PACK, CUT_2, N)
        round_y(nc.scalar.copy, CUT_2, CUT_3)
        quantise_y(0, CUT_1)
        round_y(nc.vector.tensor_copy, CUT_3, N)
        quantise_y(CUT_1, CUT_2)
        store_words(0, CUT_2)
        quantise_y(CUT_2, N)
        store_words(CUT_2, N)

        for q in range(QUADS):
            queue = nc.sync if q % 2 == 0 else nc.scalar
            queue.dma_start(out=out_2[0, rows(q), :].bitcast(I32), in_=o_sc[live(q), :].bitcast(I32))
